import numpy as np
import ml_dtypes

BF16 = ml_dtypes.bfloat16


def bf(x):
    return np.asarray(x, np.float32).astype(BF16)


def f32(x):
    return np.asarray(x, np.float32)


def f64(x):
    return np.asarray(x).astype(np.float64)


def striped(idx):
    return np.concatenate([l.reshape(-1, 16).T for l in idx])


def rows(idx, k):
    return np.tile(np.repeat(idx, 16, axis=0), (k // (16 * 8), 1))


def look(tab, idx):
    return np.take_along_axis(f64(tab), rows(idx, len(tab)), axis=1)


K, S, V, N = 256, 2048, 512, 512


def setup_inputs():
    return {"tab": f32(np.random.standard_normal((K, S))), "y": f32(np.random.standard_normal((K, V))), "offs": striped(np.stack([np.random.permutation(S)[:N] for _ in range(8)]))}


def reference(tab, y, offs):
    idx = np.stack([g.T.reshape(-1) for g in np.split(offs, 8)])
    t = look(tab, idx)
    x = t**2 * f64(y)
    return x

@@ -1,0 +1,27 @@
+import concourse.mybir as mybir
+
+P = 128
+F32 = mybir.dt.float32
+U16 = mybir.dt.uint16
+
+
+def tile_lookup_gate_sq_out_kernel(tc, tab, y, offs, out):
+    nc = tc.nc
+    rows, columns = tab.shape
+    picks = y.shape[1]
+    blocks = rows // P
+    with tc.tile_pool(name="held", bufs=1) as held:
+        offsets = held.tile([P, picks // 16], U16, name="offsets")
+        nc.sync.dma_start(offsets[:], offs)
+        windows = [held.tile([P, columns], F32, name=f"window{b}") for b in range(blocks)]
+        streams = [held.tile([P, picks], F32, name=f"stream{b}") for b in range(blocks)]
+        for b in range(blocks):
+            nc.sync.dma_start(windows[b][:], tab[b * P:(b + 1) * P, :])
+        for b in range(blocks):
+            nc.sync.dma_start(streams[b][:], y[b * P:(b + 1) * P, :])
+        for b in range(blocks):
+            squares = held.tile([P, picks], F32, name=f"squares{b}")
+            nc.scalar.activation(squares[:], windows[b][:].indirect(offsets[:]), mybir.ActivationFunctionType.Square)
+            gated = held.tile([P, picks], F32, name=f"gated{b}")
+            nc.vector.tensor_tensor(gated[:], squares[:], streams[b][:], mybir.AluOpType.mult)
+            nc.sync.dma_start(out[b * P:(b + 1) * P, :], gated[:])

@@ -19,6 +19,10 @@ def tile_lookup_gate_sq_out_kernel(tc, tab, y, offs, out):
             nc.sync.dma_start(windows[b][:], tab[b * P:(b + 1) * P, :])
         for b in range(blocks):
             nc.sync.dma_start(streams[b][:], y[b * P:(b + 1) * P, :])
+        warm_in = held.tile([P, 1], F32, name="warm_in")
+        warm_out = held.tile([P, 1], F32, name="warm_out")
+        nc.vector.memset(warm_in[:], 0.0)
+        nc.scalar.activation(warm_out[:], warm_in[:], mybir.ActivationFunctionType.Square)
         for b in range(blocks):
             squares = held.tile([P, picks], F32, name=f"squares{b}")
             nc.scalar.activation(squares[:], windows[b][:].indirect(offsets[:]), mybir.ActivationFunctionType.Square)

import concourse.mybir as mybir

P = 128
F32 = mybir.dt.float32
U16 = mybir.dt.uint16


def tile_lookup_gate_sq_out_kernel(tc, tab, y, offs, out):
    nc = tc.nc
    rows, columns = tab.shape
    picks = y.shape[1]
    blocks = rows // P
    with tc.tile_pool(name="held", bufs=1) as held:
        offsets = held.tile([P, picks // 16], U16, name="offsets")
        nc.sync.dma_start(offsets[:], offs)
        windows = [held.tile([P, columns], F32, name=f"window{b}") for b in range(blocks)]
        streams = [held.tile([P, picks], F32, name=f"stream{b}") for b in range(blocks)]
        for b in range(blocks):
            nc.sync.dma_start(windows[b][:], tab[b * P:(b + 1) * P, :])
        for b in range(blocks):
            nc.sync.dma_start(streams[b][:], y[b * P:(b + 1) * P, :])
        warm_in = held.tile([P, 1], F32, name="warm_in")
        warm_out = held.tile([P, 1], F32, name="warm_out")
        nc.vector.memset(warm_in[:], 0.0)
        nc.scalar.activation(warm_out[:], warm_in[:], mybir.ActivationFunctionType.Square)
        for b in range(blocks):
            squares = held.tile([P, picks], F32, name=f"squares{b}")
            nc.scalar.activation(squares[:], windows[b][:].indirect(offsets[:]), mybir.ActivationFunctionType.Square)
            gated = held.tile([P, picks], F32, name=f"gated{b}")
            nc.vector.tensor_tensor(gated[:], squares[:], streams[b][:], mybir.AluOpType.mult)
            nc.sync.dma_start(out[b * P:(b + 1) * P, :], gated[:])
